import numpy as np
import ml_dtypes


def mxq(x, axis, fmt="e4m3"):
    dtype, down = {"e4m3": (ml_dtypes.float8_e4m3fn, 7), "e5m2": (ml_dtypes.float8_e5m2, 14)}[fmt]
    v = np.moveaxis(np.asarray(x, np.float32).astype(ml_dtypes.bfloat16).astype(np.float64), axis, -1)
    blocks = v.reshape(v.shape[:-1] + (-1, 32))
    amax = np.abs(blocks).max(-1, keepdims=True)
    byte = np.maximum(np.where(amax > 0, np.frexp(amax)[1] - 1 + 127, 0) - down, 1)
    scale = np.exp2(byte - 127.0)
    codes = (blocks / scale).astype(np.float32).astype(dtype).astype(np.float64)
    return np.moveaxis((codes * scale).reshape(v.shape), -1, axis)


WIDE = False


def mx_kscale(k):
    if not WIDE:
        return np.ones(k)
    levels = np.array([10, -10, 5, -5, 0])
    if k % 512:
        return np.exp2(np.random.permutation(np.resize(levels, k // 32))).repeat(32)
    a = np.empty((k // 512, 16))
    for p in range(k // 512):
        a[p, :8] = np.random.permutation(np.resize(levels, 8))
        for g in range(8):
            far = levels[np.abs(levels - a[p, g]) >= 10]
            a[p, g + 8] = far[np.random.randint(len(far))]
    return np.exp2(a.ravel()).repeat(32)


def f64(x):
    return np.asarray(x).astype(np.float64)


def striped(idx):
    return np.tile(idx.reshape(-1, 16).T, (8, 1)).astype(np.uint16)


def unstriped(offs):
    return offs[:16].T.reshape(-1).astype(np.int64)


E2M1 = np.array([0.0, 0.5, 1.0, 1.5, 2.0, 3.0, 4.0, 6.0, -0.0, -0.5, -1.0, -1.5, -2.0, -3.0, -4.0, -6.0])


def pack_weight(w, fmt):
    k, n = w.shape
    w = f64(np.asarray(w, np.float32).astype(ml_dtypes.bfloat16)).reshape(k // 32, 32, n)
    amax = np.abs(w).max(1)
    if fmt == "e4m3":
        byte = np.frexp(amax)[1] - 1 + 127 - 7
    else:
        mant, ex = np.frexp(amax / 6.0)
        byte = np.where(mant > 0.5, ex, ex - 1) + 127
    byte = np.clip(np.where(amax > 0, byte, 1), 1, 254)
    scaled = (w * np.exp2(127.0 - byte)[:, None, :]).reshape(k, n).astype(np.float32)
    by_word = np.ascontiguousarray(scaled.reshape(k // 512, 128, 4, n).transpose(0, 1, 3, 2))
    if fmt == "e4m3":
        words = by_word.astype(ml_dtypes.float8_e4m3fn).view(np.uint8)
    else:
        c = by_word.astype(ml_dtypes.float4_e2m1fn).view(np.uint8) & 0xF
        words = (c[..., 0::2] | (c[..., 1::2] << 4)).reshape(k // 512, 128, 2 * n)
    return np.ascontiguousarray(words), np.ascontiguousarray(byte.astype(np.uint8).reshape(k // 512, 16, n))


def unpack_weight(words, scales, fmt):
    g, _, n = scales.shape
    words = np.ascontiguousarray(words).reshape(g, 128, n, -1)
    if fmt == "e4m3":
        vals = words.view(ml_dtypes.float8_e4m3fn).astype(np.float64)
    else:
        nib = np.empty((g, 128, n, 4), np.uint8)
        nib[..., 0::2] = words & 0xF
        nib[..., 1::2] = words >> 4
        vals = E2M1[nib]
    vals = vals * np.repeat(np.exp2(scales.astype(np.float64) - 127.0), 8, axis=1)[..., None]
    return vals.transpose(0, 1, 3, 2).reshape(g * 512, n)


K, T, E, C, N = 128, 768, 12, 128, 1024


def by_expert(wq, xq):
    return np.concatenate([wq[e].T @ xq[:, e * C:(e + 1) * C] for e in range(E)], axis=1)


def setup_inputs():
    n = np.random.standard_normal
    s = mx_kscale(N)[:, None]
    first = np.random.permutation(np.repeat(np.arange(E), T // E))
    second = (first + 1 + np.random.permutation(np.repeat(np.arange(E - 1), -(-T // (E - 1)))[:T])) % E
    while np.bincount(second, minlength=E).max() != T // E:
        load = np.bincount(second, minlength=E); hi, lo = int(load.argmax()), int(load.argmin())
        t = np.flatnonzero((second == hi) & (first != lo))[0]; second[t] = lo
    slot_token = np.empty(E * C, np.int64); pos = np.empty((2, T), np.int64); fill = np.zeros(E, np.int64)
    place = np.stack([np.random.permutation(C) for _ in range(E)])
    for r, deal in enumerate((first, second)):
        for t in np.random.permutation(T):
            e = deal[t]; j = e * C + place[e, fill[e]]; fill[e] += 1; slot_token[j] = t; pos[r, t] = j
    g = np.random.uniform(0.2, 0.8, T)
    w_slot = np.empty(E * C); w_slot[pos[0]] = g; w_slot[pos[1]] = 1.0 - g
    w = [pack_weight(m, "e2m1") for m in n((E, N, K)) / np.sqrt(N) / s[None]]
    return {
        "dyT": (n((N, T)) * s).astype(np.float32),
        "w_words": np.stack([m[0] for m in w]),
        "w_scales": np.stack([m[1] for m in w]),
        "gate": np.tile(w_slot, (N, 1)).astype(np.float32),
        "offs": striped(slot_token),
        "pos1": striped(pos[0]),
        "pos2": striped(pos[1]),
    }


def reference(dyT, w_words, w_scales, gate, offs, pos1, pos2):
    idx = unstriped(offs)
    w = np.stack([unpack_weight(w_words[e], w_scales[e], "e2m1") for e in range(E)])
    gq = mxq(f64(gate) * f64(dyT)[:, idx], 0, "e4m3")
    dx = by_expert(w, gq)
    return dx[:, unstriped(pos1)] + dx[:, unstriped(pos2)]

@@ -1,0 +1,154 @@
+from contextlib import ExitStack
+
+import concourse.mybir as mybir
+
+F32 = mybir.dt.float32
+BF16 = mybir.dt.bfloat16
+U32 = mybir.dt.uint32
+I32 = mybir.dt.int32
+U16 = mybir.dt.uint16
+U8 = mybir.dt.uint8
+FP8X4 = mybir.dt.float8_e4m3fn_x4
+FP4X4 = mybir.dt.float4_e2m1fn_x4
+MULT = mybir.AluOpType.mult
+
+P = 128
+K, T, E, C, N = 128, 768, 12, 128, 1024
+S = E * C
+PASSES = N // 512
+PACK = 4
+
+FLOPS = 2 * N * K * S
+BYTES = 4 * N * T + E * N * K // 2 + E * N * K // 32 + 4 * S + 2 * P * (S + 2 * T) // 16 + 4 * K * T
+
+CHUNK = 512
+PER_CHUNK = CHUNK // C
+
+
+def tile_moe_bdx_lin_none_kernel(tc, dyT, w_words, w_scales, gate, offs, pos1, pos2, out):
+    nc = tc.nc
+    with ExitStack() as ctx:
+        lists = ctx.enter_context(tc.tile_pool(name="lists", bufs=1))
+        keep = ctx.enter_context(tc.tile_pool(name="keep", bufs=1))
+        psum = ctx.enter_context(tc.psum_pool(name="psum", bufs=1))
+
+        offs_sb = lists.tile([P, S // 16], U16, name="offs_sb")
+        pos1_sb = lists.tile([P, T // 16], U16, name="pos1_sb")
+        pos2_sb = lists.tile([P, T // 16], U16, name="pos2_sb")
+
+        w_sb = keep.tile([P, E * PASSES, 2 * K], U8, name="w_sb", align_bytes=64)
+        ws_sb = keep.tile([P, E * PASSES, K], U8, name="ws_sb", align_bytes=64)
+        gate_sb = keep.tile([P, S], F32, name="gate_sb")
+        planes = [[keep.tile([P, T], F32, name=f"dy_{a}_{d}") for d in range(PACK)] for a in range(PASSES)]
+        dx = keep.tile([P, S], F32, name="dx")
+
+        rows = dyT.rearrange("(a p d) t -> a d p t", a=PASSES, d=PACK)
+        nc.sync.dma_start(offs_sb[:], offs)
+        nc.scalar.dma_start(out=gate_sb[:, 0:256], in_=gate[0:P, 0:256])
+        nc.sync.dma_start(out=planes[0][0][:], in_=rows[0, 0])
+        nc.scalar.dma_start(out=gate_sb[:, 256:512], in_=gate[0:P, 256:512])
+        for a in range(PASSES):
+            for d in range(PACK):
+                if a + d > 0:
+                    nc.sync.dma_start(out=planes[a][d][:], in_=rows[a, d])
+        nc.sync.dma_start(out=gate_sb[:, 512:1024], in_=gate[0:P, 512:1024])
+        nc.vector.memset(ws_sb[:].rearrange("p g k -> p (g k)").bitcast(I32), 0)
+        words = w_words.bitcast(I32).rearrange("e a p n -> p (e a) n")
+        w_i32 = w_sb[:].bitcast(I32)
+        half = E * PASSES // 2
+        nc.sync.dma_start(out=w_i32[:, 0:half, :], in_=words[:, 0:half, :])
+        scale_rows = w_scales.bitcast(I32).rearrange("e a f k -> f (e a) k")
+        ws_i32 = ws_sb[:].bitcast(I32)
+        for q in range(4):
+            nc.sync.dma_start(out=ws_i32[32 * q : 32 * q + 4, :, :], in_=scale_rows[4 * q : 4 * q + 4, :, :])
+        nc.sync.dma_start(out=gate_sb[:, 1024:S], in_=gate[0:P, 1024:S])
+        nc.sync.dma_start(out=w_i32[:, half:, :], in_=words[:, half:, :])
+        nc.sync.dma_start(pos1_sb[:], pos1)
+        nc.sync.dma_start(pos2_sb[:], pos2)
+
+        for c in range(S // CHUNK):
+            g4 = [keep.tile([P, PACK, CHUNK], F32, name=f"g4_{c}_{a}") for a in range(PASSES)]
+            gb = [keep.tile([P, CHUNK * PACK], BF16, name=f"gb_{c}_{a}", align_bytes=64) for a in range(PASSES)]
+            codes = [keep.tile([P, CHUNK], U32, name=f"codes_{c}_{a}", align_bytes=64) for a in range(PASSES)]
+            scales = [keep.tile([P, CHUNK], U8, name=f"scales_{c}_{a}", align_bytes=64) for a in range(PASSES)]
+
+            def gather(a, d, lo, hi):
+                first, last = c * CHUNK + lo, c * CHUNK + hi
+                nc.vector.tensor_tensor(
+                    g4[a][:, d, lo:hi],
+                    planes[a][d][:].indirect(offs_sb[:, first // 16 : last // 16]),
+                    gate_sb[:, first:last],
+                    MULT,
+                )
+
+            def interleave(a, lo, hi, engine):
+                dst = gb[a][:, PACK * lo : PACK * hi].rearrange("p (n d) -> p n d", d=PACK)
+                src = g4[a][:, :, lo:hi].rearrange("p d n -> p n d")
+                if engine == "scalar":
+                    nc.scalar.copy(dst, src)
+                else:
+                    nc.vector.tensor_copy(dst, src)
+
+            def quantise(a, lo, hi):
+                nc.vector.quantize_mx(
+                    out=codes[a][:, lo:hi].bitcast(FP8X4),
+                    scales=scales[a][:, lo:hi],
+                    in_=gb[a][:, PACK * lo : PACK * hi],
+                )
+
+            def multiply(bank, e, at):
+                cols = slice(e * C - c * CHUNK, (e + 1) * C - c * CHUNK)
+                for a in range(PASSES):
+                    nc.tensor.matmul_mx(
+                        out=bank[:, at : at + C],
+                        lhsT=w_sb[:, PASSES * e + a, :].bitcast(FP4X4),
+                        lhsT_scale=ws_sb[:, PASSES * e + a, :],
+                        rhs=codes[a][:, cols].bitcast(FP8X4),
+                        rhs_scale=scales[a][:, cols],
+                        start=(a == 0),
+                        stop=(a == PASSES - 1),
+                    )
+
+            if c < 2:
+                for a in range(PASSES):
+                    for d in range(PACK):
+                        if c + a + d == 0:
+                            gather(a, d, 0, 256)
+                            gather(a, d, 256, CHUNK)
+                        else:
+                            gather(a, d, 0, CHUNK)
+                    interleave(a, 0, CHUNK, "scalar")
+                    quantise(a, 0, CHUNK)
+                bank = psum.tile([P, CHUNK], F32, name=f"bank_{c}")
+                for i in range(PER_CHUNK):
+                    multiply(bank, c * PER_CHUNK + i, i * C)
+                nc.scalar.copy(dx[:, c * CHUNK : (c + 1) * CHUNK], bank[:])
+            else:
+                for d in range(PACK):
+                    gather(0, d, 0, CHUNK)
+                interleave(0, 0, CHUNK, "scalar")
+                quantise(0, 0, CHUNK)
+                for lo, hi, engine in ((0, 256, "scalar"), (256, 384, "scalar"), (384, 448, "scalar"), (448, 512, "vector")):
+                    for d in range(PACK):
+                        gather(1, d, lo, hi)
+                    interleave(1, lo, hi, engine)
+                    quantise(1, lo, hi)
+                    if hi == 448:
+                        continue
+                    first, last = lo // C, hi // C
+                    bank = psum.tile([P, CHUNK], F32, name=f"bank_{c}_{lo}")
+                    for e in range(first, last):
+                        multiply(bank, c * PER_CHUNK + e, (e - first) * C)
+                    if hi < CHUNK:
+                        nc.scalar.copy(dx[:, c * CHUNK + lo : c * CHUNK + hi], bank[:, 0 : hi - lo])
+                    else:
+                        nc.vector.tensor_copy(dx[:, S - C : S], bank[:, 0:C])
+
+        one = keep.tile([P, T], F32, name="one")
+        two = keep.tile([P, T], F32, name="two")
+        both = keep.tile([P, T], F32, name="both")
+        nc.vector.tensor_copy(one[:], dx[:].indirect(pos1_sb[:]))
+        for lo, hi in ((0, 512), (512, T)):
+            nc.vector.tensor_copy(two[:, lo:hi], dx[:].indirect(pos2_sb[:, lo // 16 : hi // 16]))
+            nc.vector.tensor_tensor(both[:, lo:hi], one[:, lo:hi], two[:, lo:hi], mybir.AluOpType.add)
+            nc.sync.dma_start(out=out[:, lo:hi], in_=both[:, lo:hi])

@@ -22,7 +22,7 @@ FLOPS = 2 * N * K * S
 BYTES = 4 * N * T + E * N * K // 2 + E * N * K // 32 + 4 * S + 2 * P * (S + 2 * T) // 16 + 4 * K * T
 
 CHUNK = 512
-PER_CHUNK = CHUNK // C
+LAG = (1, 1, 1, 1, 1, 2, 2, 2, 2)
 
 
 def tile_moe_bdx_lin_none_kernel(tc, dyT, w_words, w_scales, gate, offs, pos1, pos2, out):
@@ -66,83 +66,82 @@ def tile_moe_bdx_lin_none_kernel(tc, dyT, w_words, w_scales, gate, offs, pos1, p
         nc.sync.dma_start(pos1_sb[:], pos1)
         nc.sync.dma_start(pos2_sb[:], pos2)
 
-        for c in range(S // CHUNK):
-            g4 = [keep.tile([P, PACK, CHUNK], F32, name=f"g4_{c}_{a}") for a in range(PASSES)]
-            gb = [keep.tile([P, CHUNK * PACK], BF16, name=f"gb_{c}_{a}", align_bytes=64) for a in range(PASSES)]
-            codes = [keep.tile([P, CHUNK], U32, name=f"codes_{c}_{a}", align_bytes=64) for a in range(PASSES)]
-            scales = [keep.tile([P, CHUNK], U8, name=f"scales_{c}_{a}", align_bytes=64) for a in range(PASSES)]
+        chunks = S // CHUNK
+        g4, gb, codes, scales = {}, {}, {}, {}
+        for c in range(chunks):
+            for a in range(PASSES):
+                g4[c, a] = keep.tile([P, PACK, CHUNK], F32, name=f"g4_{c}_{a}")
+                gb[c, a] = keep.tile([P, CHUNK * PACK], BF16, name=f"gb_{c}_{a}", align_bytes=64)
+                codes[c, a] = keep.tile([P, CHUNK], U32, name=f"codes_{c}_{a}", align_bytes=64)
+                scales[c, a] = keep.tile([P, CHUNK], U8, name=f"scales_{c}_{a}", align_bytes=64)
 
-            def gather(a, d, lo, hi):
-                first, last = c * CHUNK + lo, c * CHUNK + hi
-                nc.vector.tensor_tensor(
-                    g4[a][:, d, lo:hi],
-                    planes[a][d][:].indirect(offs_sb[:, first // 16 : last // 16]),
-                    gate_sb[:, first:last],
-                    MULT,
-                )
+        def gather(c, a, d, lo, hi):
+            first, last = c * CHUNK + lo, c * CHUNK + hi
+            nc.vector.tensor_tensor(
+                g4[c, a][:, d, lo:hi],
+                planes[a][d][:].indirect(offs_sb[:, first // 16 : last // 16]),
+                gate_sb[:, first:last],
+                MULT,
+            )
 
-            def interleave(a, lo, hi, engine):
-                dst = gb[a][:, PACK * lo : PACK * hi].rearrange("p (n d) -> p n d", d=PACK)
-                src = g4[a][:, :, lo:hi].rearrange("p d n -> p n d")
-                if engine == "scalar":
-                    nc.scalar.copy(dst, src)
-                else:
-                    nc.vector.tensor_copy(dst, src)
+        def interleave(copy, c, a, lo, hi):
+            copy(
+                gb[c, a][:, PACK * lo : PACK * hi].rearrange("p (n d) -> p n d", d=PACK),
+                g4[c, a][:, :, lo:hi].rearrange("p d n -> p n d"),
+            )
 
-            def quantise(a, lo, hi):
-                nc.vector.quantize_mx(
-                    out=codes[a][:, lo:hi].bitcast(FP8X4),
-                    scales=scales[a][:, lo:hi],
-                    in_=gb[a][:, PACK * lo : PACK * hi],
-                )
+        def quantise(c, a, lo, hi):
+            nc.vector.quantize_mx(
+                out=codes[c, a][:, lo:hi].bitcast(FP8X4),
+                scales=scales[c, a][:, lo:hi],
+                in_=gb[c, a][:, PACK * lo : PACK * hi],
+            )
 
-            def multiply(bank, e, at):
-                cols = slice(e * C - c * CHUNK, (e + 1) * C - c * CHUNK)
+        def multiply(copy, c, lo, hi):
+            bank = psum.tile([P, CHUNK], F32, name=f"bank_{c}_{lo}")
+            for at in range(lo, hi, C):
+                e = (c * CHUNK + at) // C
                 for a in range(PASSES):
                     nc.tensor.matmul_mx(
-                        out=bank[:, at : at + C],
+                        out=bank[:, at - lo : at - lo + C],
                         lhsT=w_sb[:, PASSES * e + a, :].bitcast(FP4X4),
                         lhsT_scale=ws_sb[:, PASSES * e + a, :],
-                        rhs=codes[a][:, cols].bitcast(FP8X4),
-                        rhs_scale=scales[a][:, cols],
+                        rhs=codes[c, a][:, at : at + C].bitcast(FP8X4),
+                        rhs_scale=scales[c, a][:, at : at + C],
                         start=(a == 0),
                         stop=(a == PASSES - 1),
                     )
+            copy(dx[:, c * CHUNK + lo : c * CHUNK + hi], bank[:, 0 : hi - lo])
 
-            if c < 2:
-                for a in range(PASSES):
-                    for d in range(PACK):
-                        if c + a + d == 0:
-                            gather(a, d, 0, 256)
-                            gather(a, d, 256, CHUNK)
-                        else:
-                            gather(a, d, 0, CHUNK)
-                    interleave(a, 0, CHUNK, "scalar")
-                    quantise(a, 0, CHUNK)
-                bank = psum.tile([P, CHUNK], F32, name=f"bank_{c}")
-                for i in range(PER_CHUNK):
-                    multiply(bank, c * PER_CHUNK + i, i * C)
-                nc.scalar.copy(dx[:, c * CHUNK : (c + 1) * CHUNK], bank[:])
-            else:
-                for d in range(PACK):
-                    gather(0, d, 0, CHUNK)
-                interleave(0, 0, CHUNK, "scalar")
-                quantise(0, 0, CHUNK)
-                for lo, hi, engine in ((0, 256, "scalar"), (256, 384, "scalar"), (384, 448, "scalar"), (448, 512, "vector")):
-                    for d in range(PACK):
-                        gather(1, d, lo, hi)
-                    interleave(1, lo, hi, engine)
-                    quantise(1, lo, hi)
-                    if hi == 448:
-                        continue
-                    first, last = lo // C, hi // C
-                    bank = psum.tile([P, CHUNK], F32, name=f"bank_{c}_{lo}")
-                    for e in range(first, last):
-                        multiply(bank, c * PER_CHUNK + e, (e - first) * C)
-                    if hi < CHUNK:
-                        nc.scalar.copy(dx[:, c * CHUNK + lo : c * CHUNK + hi], bank[:, 0 : hi - lo])
-                    else:
-                        nc.vector.tensor_copy(dx[:, S - C : S], bank[:, 0:C])
+        pieces = [(c, a, 0, CHUNK) for c in range(chunks) for a in range(PASSES)][:-1]
+        pieces += [(chunks - 1, 1, lo, hi) for lo, hi in ((0, 256), (256, 384), (384, 448), (448, 512))]
+
+        def finish(piece):
+            quantise(*piece)
+            c, a, lo, hi = piece
+            if a == 1 and hi % C == 0:
+                lo = lo // C * C
+                multiply(nc.vector.tensor_copy if c * CHUNK + hi == S else nc.scalar.copy, c, lo, hi)
+
+        done = 0
+        for i, (c, a, lo, hi) in enumerate(pieces):
+            for d in range(PACK):
+                if i + d == 0:
+                    gather(c, a, d, 0, 256)
+                    gather(c, a, d, 256, CHUNK)
+                else:
+                    gather(c, a, d, lo, hi)
+            last = i == len(pieces) - 1
+            if last:
+                finish(pieces[done])
+            interleave(nc.vector.tensor_copy if last else nc.scalar.copy, c, a, lo, hi)
+            if last:
+                finish(pieces[done + 1])
+                finish(pieces[i])
+            elif i >= LAG[i]:
+                while done <= i - LAG[i]:
+                    finish(pieces[done])
+                    done += 1
 
         one = keep.tile([P, T], F32, name="one")
         two = keep.tile([P, T], F32, name="two")

@@ -21,8 +21,10 @@ PACK = 4
 FLOPS = 2 * N * K * S
 BYTES = 4 * N * T + E * N * K // 2 + E * N * K // 32 + 4 * S + 2 * P * (S + 2 * T) // 16 + 4 * K * T
 
-CHUNK = 512
-LAG = (1, 1, 1, 1, 1, 2, 2, 2, 2)
+CHUNK = S // 2
+WIDE = T + 8
+
+PIECES = ((0, 0, 0, 768), (0, 1, 0, 768), (1, 0, 0, 768), (1, 1, 0, 384), (1, 1, 384, 640), (1, 1, 640, 768))
 
 
 def tile_moe_bdx_lin_none_kernel(tc, dyT, w_words, w_scales, gate, offs, pos1, pos2, out):
@@ -39,19 +41,29 @@ def tile_moe_bdx_lin_none_kernel(tc, dyT, w_words, w_scales, gate, offs, pos1, p
         w_sb = keep.tile([P, E * PASSES, 2 * K], U8, name="w_sb", align_bytes=64)
         ws_sb = keep.tile([P, E * PASSES, K], U8, name="ws_sb", align_bytes=64)
         gate_sb = keep.tile([P, S], F32, name="gate_sb")
-        planes = [[keep.tile([P, T], F32, name=f"dy_{a}_{d}") for d in range(PACK)] for a in range(PASSES)]
+        last_plane = (PASSES - 1, PACK - 1)
+        planes = {}
+        for a in range(PASSES):
+            for d in range(PACK):
+                planes[a, d] = keep.tile([P, T if (a, d) == last_plane else WIDE], F32, name=f"dy_{a}_{d}")
         dx = keep.tile([P, S], F32, name="dx")
 
-        rows = dyT.rearrange("(a p d) t -> a d p t", a=PASSES, d=PACK)
+        def load_plane(a, d):
+            skip = d if a == 0 else 0
+            rows = dyT[512 * a + skip : 512 * (a + 1) + skip, :]
+            width = planes[a, d].shape[1]
+            at = (d - skip) * T
+            four = rows.rearrange("(p r) t -> p (r t)", r=PACK)
+            nc.sync.dma_start(out=planes[a, d][:], in_=four[:, at : at + width])
+
         nc.sync.dma_start(offs_sb[:], offs)
         nc.scalar.dma_start(out=gate_sb[:, 0:256], in_=gate[0:P, 0:256])
-        nc.sync.dma_start(out=planes[0][0][:], in_=rows[0, 0])
-        nc.scalar.dma_start(out=gate_sb[:, 256:512], in_=gate[0:P, 256:512])
+        load_plane(0, 0)
+        nc.sync.dma_start(out=gate_sb[:, 256:CHUNK], in_=gate[0:P, 256:CHUNK])
         for a in range(PASSES):
             for d in range(PACK):
                 if a + d > 0:
-                    nc.sync.dma_start(out=planes[a][d][:], in_=rows[a, d])
-        nc.sync.dma_start(out=gate_sb[:, 512:1024], in_=gate[0:P, 512:1024])
+                    load_plane(a, d)
         nc.vector.memset(ws_sb[:].rearrange("p g k -> p (g k)").bitcast(I32), 0)
         words = w_words.bitcast(I32).rearrange("e a p n -> p (e a) n")
         w_i32 = w_sb[:].bitcast(I32)
@@ -61,14 +73,13 @@ def tile_moe_bdx_lin_none_kernel(tc, dyT, w_words, w_scales, gate, offs, pos1, p
         ws_i32 = ws_sb[:].bitcast(I32)
         for q in range(4):
             nc.sync.dma_start(out=ws_i32[32 * q : 32 * q + 4, :, :], in_=scale_rows[4 * q : 4 * q + 4, :, :])
-        nc.sync.dma_start(out=gate_sb[:, 1024:S], in_=gate[0:P, 1024:S])
+        nc.sync.dma_start(out=gate_sb[:, CHUNK:S], in_=gate[0:P, CHUNK:S])
         nc.sync.dma_start(out=w_i32[:, half:, :], in_=words[:, half:, :])
         nc.sync.dma_start(pos1_sb[:], pos1)
         nc.sync.dma_start(pos2_sb[:], pos2)
 
-        chunks = S // CHUNK
         g4, gb, codes, scales = {}, {}, {}, {}
-        for c in range(chunks):
+        for c in range(S // CHUNK):
             for a in range(PASSES):
                 g4[c, a] = keep.tile([P, PACK, CHUNK], F32, name=f"g4_{c}_{a}")
                 gb[c, a] = keep.tile([P, CHUNK * PACK], BF16, name=f"gb_{c}_{a}", align_bytes=64)
@@ -79,7 +90,7 @@ def tile_moe_bdx_lin_none_kernel(tc, dyT, w_words, w_scales, gate, offs, pos1, p
             first, last = c * CHUNK + lo, c * CHUNK + hi
             nc.vector.tensor_tensor(
                 g4[c, a][:, d, lo:hi],
-                planes[a][d][:].indirect(offs_sb[:, first // 16 : last // 16]),
+                planes[a, d][:].indirect(offs_sb[:, first // 16 : last // 16]),
                 gate_sb[:, first:last],
                 MULT,
             )
@@ -91,14 +102,17 @@ def tile_moe_bdx_lin_none_kernel(tc, dyT, w_words, w_scales, gate, offs, pos1, p
             )
 
         def quantise(c, a, lo, hi):
-            nc.vector.quantize_mx(
-                out=codes[c, a][:, lo:hi].bitcast(FP8X4),
-                scales=scales[c, a][:, lo:hi],
-                in_=gb[c, a][:, PACK * lo : PACK * hi],
-            )
+            while lo < hi:
+                width = max(w for w in (512, 256, 128) if lo + w <= hi)
+                nc.vector.quantize_mx(
+                    out=codes[c, a][:, lo : lo + width].bitcast(FP8X4),
+                    scales=scales[c, a][:, lo : lo + width],
+                    in_=gb[c, a][:, PACK * lo : PACK * (lo + width)],
+                )
+                lo += width
 
         def multiply(copy, c, lo, hi):
-            bank = psum.tile([P, CHUNK], F32, name=f"bank_{c}_{lo}")
+            bank = psum.tile([P, 512], F32, name=f"bank_{c}_{lo}")
             for at in range(lo, hi, C):
                 e = (c * CHUNK + at) // C
                 for a in range(PASSES):
@@ -113,35 +127,29 @@ def tile_moe_bdx_lin_none_kernel(tc, dyT, w_words, w_scales, gate, offs, pos1, p
                     )
             copy(dx[:, c * CHUNK + lo : c * CHUNK + hi], bank[:, 0 : hi - lo])
 
-        pieces = [(c, a, 0, CHUNK) for c in range(chunks) for a in range(PASSES)][:-1]
-        pieces += [(chunks - 1, 1, lo, hi) for lo, hi in ((0, 256), (256, 384), (384, 448), (448, 512))]
+        def finish(c, a, lo, hi):
+            quantise(c, a, lo, hi)
+            if a < PASSES - 1:
+                return
+            step = 512 if c == 0 else C
+            for at in range(lo, hi, step):
+                end = min(at + step, hi)
+                multiply(nc.vector.tensor_copy if c * CHUNK + end == S else nc.scalar.copy, c, at, end)
 
-        def finish(piece):
-            quantise(*piece)
-            c, a, lo, hi = piece
-            if a == 1 and hi % C == 0:
-                lo = lo // C * C
-                multiply(nc.vector.tensor_copy if c * CHUNK + hi == S else nc.scalar.copy, c, lo, hi)
-
-        done = 0
-        for i, (c, a, lo, hi) in enumerate(pieces):
+        for i, (c, a, lo, hi) in enumerate(PIECES):
             for d in range(PACK):
                 if i + d == 0:
-                    gather(c, a, d, 0, 256)
-                    gather(c, a, d, 256, CHUNK)
+                    gather(c, a, d, lo, 256)
+                    gather(c, a, d, 256, hi)
+                elif (a, d) == last_plane and hi - lo == CHUNK:
+                    gather(c, a, d, lo, 512)
+                    gather(c, a, d, 512, hi)
                 else:
                     gather(c, a, d, lo, hi)
-            last = i == len(pieces) - 1
-            if last:
-                finish(pieces[done])
-            interleave(nc.vector.tensor_copy if last else nc.scalar.copy, c, a, lo, hi)
-            if last:
-                finish(pieces[done + 1])
-                finish(pieces[i])
-            elif i >= LAG[i]:
-                while done <= i - LAG[i]:
-                    finish(pieces[done])
-                    done += 1
+            interleave(nc.vector.tensor_copy if i == len(PIECES) - 1 else nc.scalar.copy, c, a, lo, hi)
+            if i > 0:
+                finish(*PIECES[i - 1])
+        finish(*PIECES[-1])
 
         one = keep.tile([P, T], F32, name="one")
         two = keep.tile([P, T], F32, name="two")

@@ -21,10 +21,21 @@ PACK = 4
 FLOPS = 2 * N * K * S
 BYTES = 4 * N * T + E * N * K // 2 + E * N * K // 32 + 4 * S + 2 * P * (S + 2 * T) // 16 + 4 * K * T
 
-CHUNK = S // 2
-WIDE = T + 8
+CHUNK = 512
+HEAD = 256
 
-PIECES = ((0, 0, 0, 768), (0, 1, 0, 768), (1, 0, 0, 768), (1, 1, 0, 384), (1, 1, 384, 640), (1, 1, 640, 768))
+PIECES = (
+    (0, 0, 0, 512, 1),
+    (0, 1, 0, 512, 1),
+    (1, 0, 0, 512, 1),
+    (1, 1, 0, 512, 2),
+    (2, 0, 0, 256, 2),
+    (2, 0, 256, 512, 2),
+    (2, 1, 0, 256, 2),
+    (2, 1, 256, 384, 2),
+    (2, 1, 384, 448, 1),
+    (2, 1, 448, 512, 0),
+)
 
 
 def tile_moe_bdx_lin_none_kernel(tc, dyT, w_words, w_scales, gate, offs, pos1, pos2, out):
@@ -41,29 +52,22 @@ def tile_moe_bdx_lin_none_kernel(tc, dyT, w_words, w_scales, gate, offs, pos1, p
         w_sb = keep.tile([P, E * PASSES, 2 * K], U8, name="w_sb", align_bytes=64)
         ws_sb = keep.tile([P, E * PASSES, K], U8, name="ws_sb", align_bytes=64)
         gate_sb = keep.tile([P, S], F32, name="gate_sb")
-        last_plane = (PASSES - 1, PACK - 1)
         planes = {}
         for a in range(PASSES):
             for d in range(PACK):
-                planes[a, d] = keep.tile([P, T if (a, d) == last_plane else WIDE], F32, name=f"dy_{a}_{d}")
+                planes[a, d] = keep.tile([P, T], F32, name=f"dy_{a}_{d}")
         dx = keep.tile([P, S], F32, name="dx")
 
-        def load_plane(a, d):
-            skip = d if a == 0 else 0
-            rows = dyT[512 * a + skip : 512 * (a + 1) + skip, :]
-            width = planes[a, d].shape[1]
-            at = (d - skip) * T
-            four = rows.rearrange("(p r) t -> p (r t)", r=PACK)
-            nc.sync.dma_start(out=planes[a, d][:], in_=four[:, at : at + width])
-
+        rows = dyT.rearrange("(a p d) t -> a d p t", a=PASSES, d=PACK)
         nc.sync.dma_start(offs_sb[:], offs)
-        nc.scalar.dma_start(out=gate_sb[:, 0:256], in_=gate[0:P, 0:256])
-        load_plane(0, 0)
-        nc.sync.dma_start(out=gate_sb[:, 256:CHUNK], in_=gate[0:P, 256:CHUNK])
+        nc.scalar.dma_start(out=gate_sb[:, 0:HEAD], in_=gate[0:P, 0:HEAD])
+        nc.sync.dma_start(out=planes[0, 0][:], in_=rows[0, 0])
+        nc.sync.dma_start(out=gate_sb[:, HEAD:CHUNK], in_=gate[0:P, HEAD:CHUNK])
         for a in range(PASSES):
             for d in range(PACK):
                 if a + d > 0:
-                    load_plane(a, d)
+                    nc.sync.dma_start(out=planes[a, d][:], in_=rows[a, d])
+        nc.sync.dma_start(out=gate_sb[:, CHUNK : 2 * CHUNK], in_=gate[0:P, CHUNK : 2 * CHUNK])
         nc.vector.memset(ws_sb[:].rearrange("p g k -> p (g k)").bitcast(I32), 0)
         words = w_words.bitcast(I32).rearrange("e a p n -> p (e a) n")
         w_i32 = w_sb[:].bitcast(I32)
@@ -73,7 +77,7 @@ def tile_moe_bdx_lin_none_kernel(tc, dyT, w_words, w_scales, gate, offs, pos1, p
         ws_i32 = ws_sb[:].bitcast(I32)
         for q in range(4):
             nc.sync.dma_start(out=ws_i32[32 * q : 32 * q + 4, :, :], in_=scale_rows[4 * q : 4 * q + 4, :, :])
-        nc.sync.dma_start(out=gate_sb[:, CHUNK:S], in_=gate[0:P, CHUNK:S])
+        nc.sync.dma_start(out=gate_sb[:, 2 * CHUNK : S], in_=gate[0:P, 2 * CHUNK : S])
         nc.sync.dma_start(out=w_i32[:, half:, :], in_=words[:, half:, :])
         nc.sync.dma_start(pos1_sb[:], pos1)
         nc.sync.dma_start(pos2_sb[:], pos2)
@@ -97,13 +101,13 @@ def tile_moe_bdx_lin_none_kernel(tc, dyT, w_words, w_scales, gate, offs, pos1, p
 
         def interleave(copy, c, a, lo, hi):
             copy(
-                gb[c, a][:, PACK * lo : PACK * hi].rearrange("p (n d) -> p n d", d=PACK),
-                g4[c, a][:, :, lo:hi].rearrange("p d n -> p n d"),
+                gb[c, a][:, PACK * lo : PACK * hi].rearrange("p (n i d) -> p n d i", d=PACK, i=4),
+                g4[c, a][:, :, lo:hi].rearrange("p d (n i) -> p n d i", i=4),
             )
 
         def quantise(c, a, lo, hi):
             while lo < hi:
-                width = max(w for w in (512, 256, 128) if lo + w <= hi)
+                width = max(w for w in (512, 256, 128, 64) if lo + w <= hi)
                 nc.vector.quantize_mx(
                     out=codes[c, a][:, lo : lo + width].bitcast(FP8X4),
                     scales=scales[c, a][:, lo : lo + width],
@@ -129,27 +133,27 @@ def tile_moe_bdx_lin_none_kernel(tc, dyT, w_words, w_scales, gate, offs, pos1, p
 
         def finish(c, a, lo, hi):
             quantise(c, a, lo, hi)
-            if a < PASSES - 1:
+            if a < PASSES - 1 or hi % C > 0:
                 return
-            step = 512 if c == 0 else C
-            for at in range(lo, hi, step):
-                end = min(at + step, hi)
-                multiply(nc.vector.tensor_copy if c * CHUNK + end == S else nc.scalar.copy, c, at, end)
+            step = C if c == 2 else CHUNK
+            for at in range(lo // C * C, hi, step):
+                last = c * CHUNK + at + step == S
+                multiply(nc.vector.tensor_copy if last else nc.scalar.copy, c, at, at + step)
 
-        for i, (c, a, lo, hi) in enumerate(PIECES):
+        done = 0
+        for i, (c, a, lo, hi, lag) in enumerate(PIECES):
             for d in range(PACK):
                 if i + d == 0:
-                    gather(c, a, d, lo, 256)
-                    gather(c, a, d, 256, hi)
-                elif (a, d) == last_plane and hi - lo == CHUNK:
-                    gather(c, a, d, lo, 512)
-                    gather(c, a, d, 512, hi)
+                    gather(c, a, d, lo, HEAD)
+                    gather(c, a, d, HEAD, hi)
                 else:
                     gather(c, a, d, lo, hi)
             interleave(nc.vector.tensor_copy if i == len(PIECES) - 1 else nc.scalar.copy, c, a, lo, hi)
-            if i > 0:
-                finish(*PIECES[i - 1])
-        finish(*PIECES[-1])
+            while done + PIECES[done][4] <= i:
+                finish(*PIECES[done][:4])
+                done += 1
+                if done == len(PIECES):
+                    break
 
         one = keep.tile([P, T], F32, name="one")
         two = keep.tile([P, T], F32, name="two")

@@ -21,20 +21,19 @@ PACK = 4
 FLOPS = 2 * N * K * S
 BYTES = 4 * N * T + E * N * K // 2 + E * N * K // 32 + 4 * S + 2 * P * (S + 2 * T) // 16 + 4 * K * T
 
-CHUNK = 512
+CHUNK = S // 2
 HEAD = 256
+WIDE = T + 16
 
 PIECES = (
-    (0, 0, 0, 512, 1),
-    (0, 1, 0, 512, 1),
-    (1, 0, 0, 512, 1),
-    (1, 1, 0, 512, 2),
-    (2, 0, 0, 256, 2),
-    (2, 0, 256, 512, 2),
-    (2, 1, 0, 256, 2),
-    (2, 1, 256, 384, 2),
-    (2, 1, 384, 448, 1),
-    (2, 1, 448, 512, 0),
+    (0, 0, 0, 768, 1),
+    (0, 1, 0, 768, 2),
+    (1, 0, 0, 384, 2),
+    (1, 0, 384, 768, 2),
+    (1, 1, 0, 384, 2),
+    (1, 1, 384, 576, 2),
+    (1, 1, 576, 704, 1),
+    (1, 1, 704, 768, 0),
 )
 
 
@@ -55,19 +54,24 @@ def tile_moe_bdx_lin_none_kernel(tc, dyT, w_words, w_scales, gate, offs, pos1, p
         planes = {}
         for a in range(PASSES):
             for d in range(PACK):
-                planes[a, d] = keep.tile([P, T], F32, name=f"dy_{a}_{d}")
+                planes[a, d] = keep.tile([P, WIDE], F32, name=f"dy_{a}_{d}")
         dx = keep.tile([P, S], F32, name="dx")
+
+        for plane in reversed([planes[a, d] for a in range(PASSES) for d in range(PACK)]):
+            nc.gpsimd.memset(plane[:, T:WIDE], 0.0)
 
         rows = dyT.rearrange("(a p d) t -> a d p t", a=PASSES, d=PACK)
         nc.sync.dma_start(offs_sb[:], offs)
         nc.scalar.dma_start(out=gate_sb[:, 0:HEAD], in_=gate[0:P, 0:HEAD])
-        nc.sync.dma_start(out=planes[0, 0][:], in_=rows[0, 0])
+        nc.sync.dma_start(out=planes[0, 0][:, 0:T], in_=rows[0, 0])
         nc.sync.dma_start(out=gate_sb[:, HEAD:CHUNK], in_=gate[0:P, HEAD:CHUNK])
         for a in range(PASSES):
             for d in range(PACK):
                 if a + d > 0:
-                    nc.sync.dma_start(out=planes[a, d][:], in_=rows[a, d])
-        nc.sync.dma_start(out=gate_sb[:, CHUNK : 2 * CHUNK], in_=gate[0:P, CHUNK : 2 * CHUNK])
+                    nc.sync.dma_start(out=planes[a, d][:, 0:T], in_=rows[a, d])
+        nc.sync.dma_start(out=gate_sb[:, CHUNK:S], in_=gate[0:P, CHUNK:S])
+        nc.sync.dma_start(pos1_sb[:], pos1)
+        nc.sync.dma_start(pos2_sb[:], pos2)
         nc.vector.memset(ws_sb[:].rearrange("p g k -> p (g k)").bitcast(I32), 0)
         words = w_words.bitcast(I32).rearrange("e a p n -> p (e a) n")
         w_i32 = w_sb[:].bitcast(I32)
@@ -77,10 +81,7 @@ def tile_moe_bdx_lin_none_kernel(tc, dyT, w_words, w_scales, gate, offs, pos1, p
         ws_i32 = ws_sb[:].bitcast(I32)
         for q in range(4):
             nc.sync.dma_start(out=ws_i32[32 * q : 32 * q + 4, :, :], in_=scale_rows[4 * q : 4 * q + 4, :, :])
-        nc.sync.dma_start(out=gate_sb[:, 2 * CHUNK : S], in_=gate[0:P, 2 * CHUNK : S])
         nc.sync.dma_start(out=w_i32[:, half:, :], in_=words[:, half:, :])
-        nc.sync.dma_start(pos1_sb[:], pos1)
-        nc.sync.dma_start(pos2_sb[:], pos2)
 
         g4, gb, codes, scales = {}, {}, {}, {}
         for c in range(S // CHUNK):
@@ -133,12 +134,13 @@ def tile_moe_bdx_lin_none_kernel(tc, dyT, w_words, w_scales, gate, offs, pos1, p
 
         def finish(c, a, lo, hi):
             quantise(c, a, lo, hi)
-            if a < PASSES - 1 or hi % C > 0:
+            if a < PASSES - 1:
                 return
-            step = C if c == 2 else CHUNK
-            for at in range(lo // C * C, hi, step):
-                last = c * CHUNK + at + step == S
-                multiply(nc.vector.tensor_copy if last else nc.scalar.copy, c, at, at + step)
+            first, last = lo // C * C, hi // C * C
+            step = 512 if c == 0 else C
+            for at in range(first, last, step):
+                end = min(at + step, last)
+                multiply(nc.vector.tensor_copy if c * CHUNK + end == S else nc.scalar.copy, c, at, end)
 
         done = 0
         for i, (c, a, lo, hi, lag) in enumerate(PIECES):

from contextlib import ExitStack

import concourse.mybir as mybir

F32 = mybir.dt.float32
BF16 = mybir.dt.bfloat16
U32 = mybir.dt.uint32
I32 = mybir.dt.int32
U16 = mybir.dt.uint16
U8 = mybir.dt.uint8
FP8X4 = mybir.dt.float8_e4m3fn_x4
FP4X4 = mybir.dt.float4_e2m1fn_x4
MULT = mybir.AluOpType.mult

P = 128
K, T, E, C, N = 128, 768, 12, 128, 1024
S = E * C
PASSES = N // 512
PACK = 4

FLOPS = 2 * N * K * S
BYTES = 4 * N * T + E * N * K // 2 + E * N * K // 32 + 4 * S + 2 * P * (S + 2 * T) // 16 + 4 * K * T

CHUNK = S // 2
HEAD = 256
WIDE = T + 16

PIECES = (
    (0, 0, 0, 768, 1),
    (0, 1, 0, 768, 2),
    (1, 0, 0, 384, 2),
    (1, 0, 384, 768, 2),
    (1, 1, 0, 384, 2),
    (1, 1, 384, 576, 2),
    (1, 1, 576, 704, 1),
    (1, 1, 704, 768, 0),
)


def tile_moe_bdx_lin_none_kernel(tc, dyT, w_words, w_scales, gate, offs, pos1, pos2, out):
    nc = tc.nc
    with ExitStack() as ctx:
        lists = ctx.enter_context(tc.tile_pool(name="lists", bufs=1))
        keep = ctx.enter_context(tc.tile_pool(name="keep", bufs=1))
        psum = ctx.enter_context(tc.psum_pool(name="psum", bufs=1))

        offs_sb = lists.tile([P, S // 16], U16, name="offs_sb")
        pos1_sb = lists.tile([P, T // 16], U16, name="pos1_sb")
        pos2_sb = lists.tile([P, T // 16], U16, name="pos2_sb")

        w_sb = keep.tile([P, E * PASSES, 2 * K], U8, name="w_sb", align_bytes=64)
        ws_sb = keep.tile([P, E * PASSES, K], U8, name="ws_sb", align_bytes=64)
        gate_sb = keep.tile([P, S], F32, name="gate_sb")
        planes = {}
        for a in range(PASSES):
            for d in range(PACK):
                planes[a, d] = keep.tile([P, WIDE], F32, name=f"dy_{a}_{d}")
        dx = keep.tile([P, S], F32, name="dx")

        for plane in reversed([planes[a, d] for a in range(PASSES) for d in range(PACK)]):
            nc.gpsimd.memset(plane[:, T:WIDE], 0.0)

        rows = dyT.rearrange("(a p d) t -> a d p t", a=PASSES, d=PACK)
        nc.sync.dma_start(offs_sb[:], offs)
        nc.scalar.dma_start(out=gate_sb[:, 0:HEAD], in_=gate[0:P, 0:HEAD])
        nc.sync.dma_start(out=planes[0, 0][:, 0:T], in_=rows[0, 0])
        nc.sync.dma_start(out=gate_sb[:, HEAD:CHUNK], in_=gate[0:P, HEAD:CHUNK])
        for a in range(PASSES):
            for d in range(PACK):
                if a + d > 0:
                    nc.sync.dma_start(out=planes[a, d][:, 0:T], in_=rows[a, d])
        nc.sync.dma_start(out=gate_sb[:, CHUNK:S], in_=gate[0:P, CHUNK:S])
        nc.sync.dma_start(pos1_sb[:], pos1)
        nc.sync.dma_start(pos2_sb[:], pos2)
        nc.vector.memset(ws_sb[:].rearrange("p g k -> p (g k)").bitcast(I32), 0)
        words = w_words.bitcast(I32).rearrange("e a p n -> p (e a) n")
        w_i32 = w_sb[:].bitcast(I32)
        half = E * PASSES // 2
        nc.sync.dma_start(out=w_i32[:, 0:half, :], in_=words[:, 0:half, :])
        scale_rows = w_scales.bitcast(I32).rearrange("e a f k -> f (e a) k")
        ws_i32 = ws_sb[:].bitcast(I32)
        for q in range(4):
            nc.sync.dma_start(out=ws_i32[32 * q : 32 * q + 4, :, :], in_=scale_rows[4 * q : 4 * q + 4, :, :])
        nc.sync.dma_start(out=w_i32[:, half:, :], in_=words[:, half:, :])

        g4, gb, codes, scales = {}, {}, {}, {}
        for c in range(S // CHUNK):
            for a in range(PASSES):
                g4[c, a] = keep.tile([P, PACK, CHUNK], F32, name=f"g4_{c}_{a}")
                gb[c, a] = keep.tile([P, CHUNK * PACK], BF16, name=f"gb_{c}_{a}", align_bytes=64)
                codes[c, a] = keep.tile([P, CHUNK], U32, name=f"codes_{c}_{a}", align_bytes=64)
                scales[c, a] = keep.tile([P, CHUNK], U8, name=f"scales_{c}_{a}", align_bytes=64)

        def gather(c, a, d, lo, hi):
            first, last = c * CHUNK + lo, c * CHUNK + hi
            nc.vector.tensor_tensor(
                g4[c, a][:, d, lo:hi],
                planes[a, d][:].indirect(offs_sb[:, first // 16 : last // 16]),
                gate_sb[:, first:last],
                MULT,
            )

        def interleave(copy, c, a, lo, hi):
            copy(
                gb[c, a][:, PACK * lo : PACK * hi].rearrange("p (n i d) -> p n d i", d=PACK, i=4),
                g4[c, a][:, :, lo:hi].rearrange("p d (n i) -> p n d i", i=4),
            )

        def quantise(c, a, lo, hi):
            while lo < hi:
                width = max(w for w in (512, 256, 128, 64) if lo + w <= hi)
                nc.vector.quantize_mx(
                    out=codes[c, a][:, lo : lo + width].bitcast(FP8X4),
                    scales=scales[c, a][:, lo : lo + width],
                    in_=gb[c, a][:, PACK * lo : PACK * (lo + width)],
                )
                lo += width

        def multiply(copy, c, lo, hi):
            bank = psum.tile([P, 512], F32, name=f"bank_{c}_{lo}")
            for at in range(lo, hi, C):
                e = (c * CHUNK + at) // C
                for a in range(PASSES):
                    nc.tensor.matmul_mx(
                        out=bank[:, at - lo : at - lo + C],
                        lhsT=w_sb[:, PASSES * e + a, :].bitcast(FP4X4),
                        lhsT_scale=ws_sb[:, PASSES * e + a, :],
                        rhs=codes[c, a][:, at : at + C].bitcast(FP8X4),
                        rhs_scale=scales[c, a][:, at : at + C],
                        start=(a == 0),
                        stop=(a == PASSES - 1),
                    )
            copy(dx[:, c * CHUNK + lo : c * CHUNK + hi], bank[:, 0 : hi - lo])

        def finish(c, a, lo, hi):
            quantise(c, a, lo, hi)
            if a < PASSES - 1:
                return
            first, last = lo // C * C, hi // C * C
            step = 512 if c == 0 else C
            for at in range(first, last, step):
                end = min(at + step, last)
                multiply(nc.vector.tensor_copy if c * CHUNK + end == S else nc.scalar.copy, c, at, end)

        done = 0
        for i, (c, a, lo, hi, lag) in enumerate(PIECES):
            for d in range(PACK):
                if i + d == 0:
                    gather(c, a, d, lo, HEAD)
                    gather(c, a, d, HEAD, hi)
                else:
                    gather(c, a, d, lo, hi)
            interleave(nc.vector.tensor_copy if i == len(PIECES) - 1 else nc.scalar.copy, c, a, lo, hi)
            while done + PIECES[done][4] <= i:
                finish(*PIECES[done][:4])
                done += 1
                if done == len(PIECES):
                    break

        one = keep.tile([P, T], F32, name="one")
        two = keep.tile([P, T], F32, name="two")
        both = keep.tile([P, T], F32, name="both")
        nc.vector.tensor_copy(one[:], dx[:].indirect(pos1_sb[:]))
        for lo, hi in ((0, 512), (512, T)):
            nc.vector.tensor_copy(two[:, lo:hi], dx[:].indirect(pos2_sb[:, lo // 16 : hi // 16]))
            nc.vector.tensor_tensor(both[:, lo:hi], one[:, lo:hi], two[:, lo:hi], mybir.AluOpType.add)
            nc.sync.dma_start(out=out[:, lo:hi], in_=both[:, lo:hi])
